import numpy as np
import ml_dtypes


def mxq(x, axis, fmt="e4m3"):
    dtype, down = {"e4m3": (ml_dtypes.float8_e4m3fn, 7), "e5m2": (ml_dtypes.float8_e5m2, 14)}[fmt]
    v = np.moveaxis(np.asarray(x, np.float32).astype(ml_dtypes.bfloat16).astype(np.float64), axis, -1)
    blocks = v.reshape(v.shape[:-1] + (-1, 32))
    amax = np.abs(blocks).max(-1, keepdims=True)
    byte = np.maximum(np.where(amax > 0, np.frexp(amax)[1] - 1 + 127, 0) - down, 1)
    scale = np.exp2(byte - 127.0)
    codes = (blocks / scale).astype(np.float32).astype(dtype).astype(np.float64)
    return np.moveaxis((codes * scale).reshape(v.shape), -1, axis)


WIDE = False


def mx_kscale(k):
    if not WIDE:
        return np.ones(k)
    levels = np.array([10, -10, 5, -5, 0])
    if k % 512:
        return np.exp2(np.random.permutation(np.resize(levels, k // 32))).repeat(32)
    a = np.empty((k // 512, 16))
    for p in range(k // 512):
        a[p, :8] = np.random.permutation(np.resize(levels, 8))
        for g in range(8):
            far = levels[np.abs(levels - a[p, g]) >= 10]
            a[p, g + 8] = far[np.random.randint(len(far))]
    return np.exp2(a.ravel()).repeat(32)


def f64(x):
    return np.asarray(x).astype(np.float64)


def striped(idx):
    return np.tile(idx.reshape(-1, 16).T, (8, 1)).astype(np.uint16)


def unstriped(offs):
    return offs[:16].T.reshape(-1).astype(np.int64)


E2M1 = np.array([0.0, 0.5, 1.0, 1.5, 2.0, 3.0, 4.0, 6.0, -0.0, -0.5, -1.0, -1.5, -2.0, -3.0, -4.0, -6.0])


def pack_weight(w, fmt):
    k, n = w.shape
    w = f64(np.asarray(w, np.float32).astype(ml_dtypes.bfloat16)).reshape(k // 32, 32, n)
    amax = np.abs(w).max(1)
    if fmt == "e4m3":
        byte = np.frexp(amax)[1] - 1 + 127 - 7
    else:
        mant, ex = np.frexp(amax / 6.0)
        byte = np.where(mant > 0.5, ex, ex - 1) + 127
    byte = np.clip(np.where(amax > 0, byte, 1), 1, 254)
    scaled = (w * np.exp2(127.0 - byte)[:, None, :]).reshape(k, n).astype(np.float32)
    by_word = np.ascontiguousarray(scaled.reshape(k // 512, 128, 4, n).transpose(0, 1, 3, 2))
    if fmt == "e4m3":
        words = by_word.astype(ml_dtypes.float8_e4m3fn).view(np.uint8)
    else:
        c = by_word.astype(ml_dtypes.float4_e2m1fn).view(np.uint8) & 0xF
        words = (c[..., 0::2] | (c[..., 1::2] << 4)).reshape(k // 512, 128, 2 * n)
    return np.ascontiguousarray(words), np.ascontiguousarray(byte.astype(np.uint8).reshape(k // 512, 16, n))


def unpack_weight(words, scales, fmt):
    g, _, n = scales.shape
    words = np.ascontiguousarray(words).reshape(g, 128, n, -1)
    if fmt == "e4m3":
        vals = words.view(ml_dtypes.float8_e4m3fn).astype(np.float64)
    else:
        nib = np.empty((g, 128, n, 4), np.uint8)
        nib[..., 0::2] = words & 0xF
        nib[..., 1::2] = words >> 4
        vals = E2M1[nib]
    vals = vals * np.repeat(np.exp2(scales.astype(np.float64) - 127.0), 8, axis=1)[..., None]
    return vals.transpose(0, 1, 3, 2).reshape(g * 512, n)


def gelu(v):
    return 0.5 * v * (1.0 + np.tanh(np.sqrt(2.0 / np.pi) * (v + 0.044715 * v**3)))


K, H, N, T, S, P = 1024, 1024, 512, 2048, 1024, 512

def setup_inputs():
    n = np.random.standard_normal
    s = mx_kscale(K)[:, None]
    u = mx_kscale(H)[:, None]
    tab_words, tab_scales = pack_weight(n((K, T)) * s, "e4m3")
    w4_words, w4_scales = pack_weight(n((H, N)) / np.sqrt(H) / u, "e2m1")
    return {
        "tab_words": tab_words,
        "tab_scales": tab_scales,
        "offs": striped(np.random.permutation(T)[:S]),
        "pos1": striped(np.random.permutation(S)[:P]),
        "pos2": striped(np.random.permutation(S)[:P]),
        "w1": (0.8 * n((K, H)) / np.sqrt(K) / s).astype(np.float32),
        "base": np.random.uniform(20, 120, H).astype(np.float32),
        "timing": (1.5 * P * n((H, P)) * u).astype(np.float32),
        "gain": (np.random.uniform(0.5, 1.5, H) * u[:, 0]).astype(np.float32),
        "w2": (n((H, N)) / np.sqrt(H) / u).astype(np.float32),
        "w4_words": w4_words,
        "w4_scales": w4_scales,
    }

def reference(tab_words, tab_scales, offs, pos1, pos2, w1, base, timing, gain, w2, w4_words, w4_scales):
    v = unpack_weight(tab_words, tab_scales, "e4m3")[:, unstriped(offs)]
    h = mxq(f64(w1), 0, "e4m3").T @ v
    top = h.max(axis=1)
    a = np.exp(h[:, unstriped(pos1)] - top[:, None])
    share = a / (f64(base)[:, None] + a.sum(axis=1)[:, None])
    d = share * f64(timing) - f64(gain)[:, None] * h[:, unstriped(pos2)]
    dq = mxq(d, 0, "e4m3")
    early = mxq(f64(w2), 0, "e4m3").T @ dq
    late = unpack_weight(w4_words, w4_scales, "e2m1").T @ dq
    return np.minimum(early, late)

@@ -1,0 +1,318 @@
+from contextlib import ExitStack
+
+import concourse.mybir as mybir
+
+K, H, N, T, S, PK = 1024, 1024, 512, 2048, 1024, 512
+FLOPS = 2 * K * H * S + 2 * 2 * H * N * PK
+
+F32 = mybir.dt.float32
+BF16 = mybir.dt.bfloat16
+I32 = mybir.dt.int32
+U32 = mybir.dt.uint32
+U16 = mybir.dt.uint16
+U8 = mybir.dt.uint8
+FP8X4 = mybir.dt.float8_e4m3fn_x4
+FP4X4 = mybir.dt.float4_e2m1fn_x4
+ALU = mybir.AluOpType
+ACT = mybir.ActivationFunctionType
+
+P = 128
+PACK = 4
+KP = P * PACK
+HALF = 256
+
+
+def tile_list_breath_peak_scores_kernel(
+    tc, tab_words, tab_scales, offs, pos1, pos2, w1, base, timing, gain, w2, w4_words, w4_scales, out
+):
+    nc = tc.nc
+    with ExitStack() as ctx:
+        keep = ctx.enter_context(tc.tile_pool(name="keep", bufs=1))
+        ring = ctx.enter_context(tc.tile_pool(name="ring", bufs=3))
+        psum = ctx.enter_context(tc.psum_pool(name="psum", bufs=4))
+
+        def held(shape, dtype, name):
+            return keep.tile(shape, dtype, name=name, align_bytes=64)
+
+        idx = keep.tile([P, S // 16], U16, name="idx")
+        p1 = keep.tile([P, PK // 16], U16, name="p1")
+        p2 = keep.tile([P, PK // 16], U16, name="p2")
+
+        tab_plane = held([P, T], U8, "tab_plane")
+        w4_plane = held([P, 2, N], U8, "w4_plane")
+        nc.vector.memset(tab_plane[:].bitcast(I32), 0)
+        nc.vector.memset(w4_plane[:].bitcast(I32), 0)
+
+        def load_tab_plane():
+            for q in range(4):
+                nc.sync.dma_start(
+                    out=tab_plane[32 * q : 32 * q + 8, :].bitcast(I32),
+                    in_=tab_scales[:, 4 * q : 4 * q + 4, :].bitcast(I32),
+                )
+
+        def load_w4_plane():
+            for q in range(4):
+                nc.sync.dma_start(
+                    out=w4_plane[32 * q : 32 * q + 4, :, :].bitcast(I32),
+                    in_=w4_scales[:, 4 * q : 4 * q + 4, :].rearrange("a r c -> r a c").bitcast(I32),
+                )
+
+        base_sb = held([P, 2, PACK], F32, "base_sb")
+        gain_sb = held([P, 2, PACK], F32, "gain_sb")
+
+        tab = [held([P, T], U32, f"tab{a}") for a in range(2)]
+        w1_raw = {(a, b, c): held([P, PACK, HALF], F32, f"w1_raw{a}{b}{c}") for a in range(2) for b in range(2) for c in range(2)}
+        w2_raw = [held([P, PACK, N], F32, f"w2_raw{b}") for b in range(2)]
+        timing_sb = [held([P, PACK, PK], F32, f"timing{b}") for b in range(2)]
+        w4_sb = held([P, 2, 2 * N], U8, "w4_sb")
+
+        def load_tab(a):
+            nc.sync.dma_start(out=tab[a][:].bitcast(I32), in_=tab_words[a].rearrange("p t i -> p (t i)").bitcast(I32))
+
+        def load_w1(a, b):
+            for c in range(2):
+                cols = slice(KP * b + HALF * c, KP * b + HALF * (c + 1))
+                nc.sync.dma_start(
+                    out=w1_raw[a, b, c][:], in_=w1[KP * a : KP * (a + 1), cols].rearrange("(p j) c -> p j c", j=PACK)
+                )
+
+        def load_rows(dst, src, b):
+            nc.sync.dma_start(out=dst[b][:], in_=src[KP * b : KP * (b + 1), :].rearrange("(p j) c -> p j c", j=PACK))
+
+        nc.sync.dma_start(idx[:], offs)
+        load_tab(0)
+        load_tab_plane()
+        load_w1(0, 0)
+        load_tab(1)
+        load_w1(1, 0)
+        nc.sync.dma_start(p1[:], pos1)
+        nc.sync.dma_start(p2[:], pos2)
+        nc.sync.dma_start(out=base_sb[:], in_=base.rearrange("(b p t) -> p b t", b=2, t=PACK))
+        nc.sync.dma_start(out=gain_sb[:], in_=gain.rearrange("(b p t) -> p b t", b=2, t=PACK))
+        load_rows(timing_sb, timing, 0)
+        load_w1(0, 1)
+        load_w1(1, 1)
+        load_rows(timing_sb, timing, 1)
+        load_rows(w2_raw, w2, 0)
+        load_rows(w2_raw, w2, 1)
+        nc.sync.dma_start(out=w4_sb[:].bitcast(I32), in_=w4_words.rearrange("a p c -> p a c").bitcast(I32))
+        load_w4_plane()
+
+        v_words = {(a, s): held([P, KP], U32, f"v_words{a}{s}") for a in range(2) for s in range(2)}
+        v_plane = [held([P, KP], U8, f"v_plane{s}") for s in range(2)]
+
+        def gather_words(a):
+            for s in range(2):
+                nc.vector.tensor_copy(v_words[a, s][:], tab[a][:].indirect(idx[:, 32 * s : 32 * (s + 1)]))
+
+        def gather_plane():
+            for s in range(2):
+                nc.vector.tensor_copy(v_plane[s][:], tab_plane[:].indirect(idx[:, 32 * s : 32 * (s + 1)]))
+
+        w1_bf = {(a, b): held([P, PACK, P, PACK], BF16, f"w1_bf{a}{b}") for a in range(2) for b in range(2)}
+        w1_codes = {(a, b): held([P, PACK, P], U32, f"w1_codes{a}{b}") for a in range(2) for b in range(2)}
+        w1_plane = {(a, b): held([P, PACK, P], U8, f"w1_plane{a}{b}") for a in range(2) for b in range(2)}
+
+        def round_w1(a, b, c, copy):
+            m0 = c * (HALF // PACK)
+            copy(
+                out=w1_bf[a, b][:, :, m0 : m0 + HALF // PACK, :].rearrange("p t m j -> p m j t"),
+                in_=w1_raw[a, b, c][:].rearrange("p j (m t) -> p m j t", t=PACK),
+            )
+
+        def quantize_w1(a, b, t0, t1):
+            nc.vector.quantize_mx(
+                out=w1_codes[a, b][:, t0:t1, :].rearrange("p t m -> p (t m)").bitcast(FP8X4),
+                scales=w1_plane[a, b][:, t0:t1, :].rearrange("p t m -> p (t m)"),
+                in_=w1_bf[a, b][:, t0:t1, :, :].rearrange("p t m j -> p (t m j)"),
+            )
+
+        neg_gain = held([P, 2, PACK], F32, "neg_gain")
+        base_part = held([P, 2, PACK], F32, "base_part")
+
+        gather_words(0)
+        round_w1(0, 0, 0, nc.scalar.copy)
+        round_w1(0, 0, 1, nc.scalar.copy)
+        gather_plane()
+        quantize_w1(0, 0, 0, 4)
+        gather_words(1)
+        round_w1(1, 0, 0, nc.scalar.copy)
+        round_w1(1, 0, 1, nc.vector.tensor_copy)
+        for t in range(PACK):
+            quantize_w1(1, 0, t, t + 1)
+        nc.scalar.mul(neg_gain[:], gain_sb[:], -1.0)
+        nc.scalar.mul(base_part[:], base_sb[:], 1.0 / PK)
+
+        d_rows = [held([P, PACK, PK], BF16, f"d_rows{b}") for b in range(2)]
+        d_bf = {(b, c): held([P, HALF, PACK], BF16, f"d_bf{b}{c}") for b in range(2) for c in range(2)}
+        d_codes = {(b, c): held([P, HALF], U32, f"d_codes{b}{c}") for b in range(2) for c in range(2)}
+        d_plane = {(b, c): held([P, HALF], U8, f"d_plane{b}{c}") for b in range(2) for c in range(2)}
+        w2_bf = [held([P, N, PACK], BF16, f"w2_bf{b}") for b in range(2)]
+        w2_codes = [held([P, N], U32, f"w2_codes{b}") for b in range(2)]
+        w2_plane = [held([P, N], U8, f"w2_plane{b}") for b in range(2)]
+
+        state = {}
+
+        def first_stage(i):
+            b, t = divmod(i, PACK)
+            banks = [psum.tile([P, KP], F32, name="h_bank", tag="h_bank") for s in range(2)]
+            for a in range(2):
+                for s in range(2):
+                    nc.tensor.matmul_mx(
+                        out=banks[s][:],
+                        lhsT=w1_codes[a, b][:, t, :].bitcast(FP8X4),
+                        lhsT_scale=w1_plane[a, b][:, t, :],
+                        rhs=v_words[a, s][:].bitcast(FP8X4),
+                        rhs_scale=v_plane[s][4 * a : P, :],
+                        start=(a == 0),
+                        stop=(a == 1),
+                    )
+            h = ring.tile([P, S], F32, name="h", bufs=4)
+            tops = held([P, 2], F32, f"tops{i}")
+            state[i] = dict(h=h, tops=tops, banks=banks)
+
+        def empty_bank(i, s):
+            st = state[i]
+            nc.vector.tensor_scalar(
+                out=st["h"][:, KP * s : KP * (s + 1)], in0=st["banks"][s][:], scalar1=1.0,
+                scalar2=(None if s == 0 else st["tops"][:, 0:1]),
+                op0=ALU.mult, op1=ALU.max, accum_out=st["tops"][:, s : s + 1],
+            )
+
+        def look(i):
+            b, t = divmod(i, PACK)
+            st = state[i]
+            neg_top = held([P, 1], F32, f"neg_top{i}")
+            nc.scalar.mul(neg_top[:], st["tops"][:, 1:2], -1.0)
+            a_look = ring.tile([P, PK], F32, name="a_look")
+            nc.scalar.activation(out=a_look[:], in_=st["h"][:].indirect(p1[:]), func=ACT.Exp, bias=neg_top[:])
+            denom = held([P, 1], F32, f"denom{i}")
+            terms = ring.tile([P, PK], BF16, name="terms", bufs=2)
+            nc.scalar.activation(
+                out=terms[:], in_=a_look[:], func=ACT.Identity, bias=base_part[:, b, t : t + 1], accum_out=denom[:]
+            )
+            st.update(a=a_look, denom=denom)
+
+        def pick(i):
+            st = state[i]
+            fasting = ring.tile([P, PK], F32, name="fasting", bufs=4)
+            nc.vector.tensor_copy(fasting[:], st["h"][:].indirect(p2[:]))
+            st.update(fasting=fasting)
+
+        def invert(i):
+            st = state[i]
+            inv = held([P, 1], F32, f"inv{i}")
+            nc.vector.reciprocal(inv[:], st["denom"][:])
+            st.update(inv=inv)
+
+        def combine(i):
+            b, t = divmod(i, PACK)
+            st = state[i]
+            inv = st["inv"]
+            timed = ring.tile([P, PK], F32, name="timed")
+            nc.vector.scalar_tensor_tensor(
+                out=timed[:], in0=st["a"][:], scalar=inv[:], in1=timing_sb[b][:, t, :], op0=ALU.mult, op1=ALU.mult
+            )
+            st.update(timed=timed)
+
+        def finish(i):
+            b, t = divmod(i, PACK)
+            st = state[i]
+            nc.vector.scalar_tensor_tensor(
+                out=d_rows[b][:, t, :], in0=st["fasting"][:], scalar=neg_gain[:, b, t : t + 1], in1=st["timed"][:],
+                op0=ALU.mult, op1=ALU.add,
+            )
+
+        def weave_d(b, c, copy):
+            copy(
+                out=d_bf[b, c][:].rearrange("p (g i) t -> p g t i", i=4),
+                in_=d_rows[b][:, :, HALF * c : HALF * (c + 1)].rearrange("p t (g i) -> p g t i", i=4),
+            )
+
+        def quantize_d(b, c):
+            nc.vector.quantize_mx(
+                out=d_codes[b, c][:].bitcast(FP8X4), scales=d_plane[b, c][:], in_=d_bf[b, c][:].rearrange("p m t -> p (m t)")
+            )
+
+        def round_w2(b, c):
+            cols = slice(HALF * c, HALF * (c + 1))
+            nc.scalar.copy(
+                out=w2_bf[b][:, cols, :].rearrange("p (g i) j -> p g j i", i=4),
+                in_=w2_raw[b][:, :, cols].rearrange("p j (g i) -> p g j i", i=4),
+            )
+
+        def quantize_w2(b):
+            nc.vector.quantize_mx(
+                out=w2_codes[b][:].bitcast(FP8X4), scales=w2_plane[b][:], in_=w2_bf[b][:].rearrange("p n j -> p (n j)")
+            )
+
+        for i in range(8 + 2):
+            if i < 8:
+                first_stage(i)
+                empty_bank(i, 0)
+            if i >= 2:
+                combine(i - 2)
+            if i < 8:
+                empty_bank(i, 1)
+                look(i)
+            if i >= 2:
+                finish(i - 2)
+            if i < 8:
+                pick(i)
+            if 1 <= i <= 8:
+                invert(i - 1)
+            if i in (0, 1):
+                round_w1(i, 1, 0, nc.scalar.copy)
+                round_w1(i, 1, 1, nc.scalar.copy)
+            if i in (1, 2):
+                quantize_w1(i - 1, 1, 0, 4)
+            if 2 <= i < 6:
+                round_w2(*divmod(i - 2, 2))
+            if i in (5, 6):
+                quantize_w2(i - 5)
+                weave_d(0, i - 5, nc.scalar.copy)
+            if i in (6, 7):
+                quantize_d(0, i - 6)
+        weave_d(1, 0, nc.vector.tensor_copy)
+        weave_d(1, 1, nc.scalar.copy)
+
+        banks = {}
+        for c in range(2):
+            for n in range(4):
+                tag = "o_bank" if c == 0 else "h_bank"
+                banks[c, n] = psum.tile([P, 2, HALF], F32, name=tag, tag=tag)
+
+        def second_stage(b, c):
+            for n in range(4):
+                cols = slice(P * n, P * (n + 1))
+                nc.tensor.matmul_mx(
+                    out=banks[c, n][:, 0, :],
+                    lhsT=w2_codes[b][:, cols].bitcast(FP8X4),
+                    lhsT_scale=w2_plane[b][:, cols],
+                    rhs=d_codes[b, c][:].bitcast(FP8X4),
+                    rhs_scale=d_plane[b, c][:],
+                    start=(b == 0),
+                    stop=False,
+                )
+                nc.tensor.matmul_mx(
+                    out=banks[c, n][:, 1, :],
+                    lhsT=w4_sb[:, b, 2 * P * n : 2 * P * (n + 1)].bitcast(FP4X4),
+                    lhsT_scale=w4_plane[:, b, cols],
+                    rhs=d_codes[b, c][:].bitcast(FP8X4),
+                    rhs_scale=d_plane[b, c][:],
+                    start=False,
+                    stop=(b == 1),
+                )
+
+        second_stage(0, 0)
+        second_stage(0, 1)
+        for c in range(2):
+            quantize_d(1, c)
+            second_stage(1, c)
+        for c in range(2):
+            for n in range(4):
+                early = ring.tile([P, HALF], F32, name="early", bufs=4)
+                nc.scalar.copy(out=early[:], in_=banks[c, n][:, 0, :])
+                score = ring.tile([P, HALF], F32, name="score", bufs=8)
+                nc.vector.tensor_tensor(out=score[:], in0=banks[c, n][:, 1, :], in1=early[:], op=ALU.min)
+                nc.sync.dma_start(out=out[P * n : P * (n + 1), HALF * c : HALF * (c + 1)], in_=score[:])

@@ -79,18 +79,18 @@ def tile_list_breath_peak_scores_kernel(
         def load_rows(dst, src, b):
             nc.sync.dma_start(out=dst[b][:], in_=src[KP * b : KP * (b + 1), :].rearrange("(p j) c -> p j c", j=PACK))
 
+        nc.scalar.dma_start(out=gain_sb[:], in_=gain.rearrange("(b p t) -> p b t", b=2, t=PACK))
+        nc.scalar.dma_start(out=base_sb[:], in_=base.rearrange("(b p t) -> p b t", b=2, t=PACK))
         nc.sync.dma_start(idx[:], offs)
         load_tab(0)
+        nc.sync.dma_start(p1[:], pos1)
         load_tab_plane()
         load_w1(0, 0)
         load_tab(1)
         load_w1(1, 0)
-        nc.sync.dma_start(p1[:], pos1)
         nc.sync.dma_start(p2[:], pos2)
-        nc.sync.dma_start(out=base_sb[:], in_=base.rearrange("(b p t) -> p b t", b=2, t=PACK))
-        nc.sync.dma_start(out=gain_sb[:], in_=gain.rearrange("(b p t) -> p b t", b=2, t=PACK))
-        load_rows(timing_sb, timing, 0)
         load_w1(0, 1)
+        load_rows(timing_sb, timing, 0)
         load_w1(1, 1)
         load_rows(timing_sb, timing, 1)
         load_rows(w2_raw, w2, 0)
@@ -130,21 +130,22 @@ def tile_list_breath_peak_scores_kernel(
         neg_gain = held([P, 2, PACK], F32, "neg_gain")
         base_part = held([P, 2, PACK], F32, "base_part")
 
+        nc.scalar.mul(neg_gain[:], gain_sb[:], -1.0)
+        nc.scalar.mul(base_part[:], base_sb[:], 1.0 / PK)
         gather_words(0)
+        gather_plane()
         round_w1(0, 0, 0, nc.scalar.copy)
         round_w1(0, 0, 1, nc.scalar.copy)
-        gather_plane()
         quantize_w1(0, 0, 0, 4)
         gather_words(1)
         round_w1(1, 0, 0, nc.scalar.copy)
         round_w1(1, 0, 1, nc.vector.tensor_copy)
         for t in range(PACK):
             quantize_w1(1, 0, t, t + 1)
-        nc.scalar.mul(neg_gain[:], gain_sb[:], -1.0)
-        nc.scalar.mul(base_part[:], base_sb[:], 1.0 / PK)
+        round_w1(0, 1, 0, nc.scalar.copy)
 
         d_rows = [held([P, PACK, PK], BF16, f"d_rows{b}") for b in range(2)]
-        d_bf = {(b, c): held([P, HALF, PACK], BF16, f"d_bf{b}{c}") for b in range(2) for c in range(2)}
+        d_bf = {}
         d_codes = {(b, c): held([P, HALF], U32, f"d_codes{b}{c}") for b in range(2) for c in range(2)}
         d_plane = {(b, c): held([P, HALF], U8, f"d_plane{b}{c}") for b in range(2) for c in range(2)}
         w2_bf = [held([P, N, PACK], BF16, f"w2_bf{b}") for b in range(2)]
@@ -184,7 +185,7 @@ def tile_list_breath_peak_scores_kernel(
             st = state[i]
             neg_top = held([P, 1], F32, f"neg_top{i}")
             nc.scalar.mul(neg_top[:], st["tops"][:, 1:2], -1.0)
-            a_look = ring.tile([P, PK], F32, name="a_look")
+            a_look = ring.tile([P, PK], F32, name="a_look", align_bytes=64)
             nc.scalar.activation(out=a_look[:], in_=st["h"][:].indirect(p1[:]), func=ACT.Exp, bias=neg_top[:])
             denom = held([P, 1], F32, f"denom{i}")
             terms = ring.tile([P, PK], BF16, name="terms", bufs=2)
@@ -224,6 +225,10 @@ def tile_list_breath_peak_scores_kernel(
             )
 
         def weave_d(b, c, copy):
+            if (b, c) == (0, 1):
+                d_bf[b, c] = ring.tile([P, HALF, PACK], BF16, name="a_look", align_bytes=64)
+            else:
+                d_bf[b, c] = held([P, HALF, PACK], BF16, f"d_bf{b}{c}")
             copy(
                 out=d_bf[b, c][:].rearrange("p (g i) t -> p g t i", i=4),
                 in_=d_rows[b][:, :, HALF * c : HALF * (c + 1)].rearrange("p t (g i) -> p g t i", i=4),
@@ -259,20 +264,22 @@ def tile_list_breath_peak_scores_kernel(
                 finish(i - 2)
             if i < 8:
                 pick(i)
-            if 1 <= i <= 8:
+            if 1 <= i < 9:
                 invert(i - 1)
-            if i in (0, 1):
-                round_w1(i, 1, 0, nc.scalar.copy)
-                round_w1(i, 1, 1, nc.scalar.copy)
+            if i == 0:
+                round_w1(0, 1, 1, nc.scalar.copy)
             if i in (1, 2):
-                quantize_w1(i - 1, 1, 0, 4)
-            if 2 <= i < 6:
-                round_w2(*divmod(i - 2, 2))
-            if i in (5, 6):
-                quantize_w2(i - 5)
-                weave_d(0, i - 5, nc.scalar.copy)
-            if i in (6, 7):
-                quantize_d(0, i - 6)
+                round_w1(1, 1, i - 1, nc.scalar.copy)
+            if i in (1, 3):
+                quantize_w1(i // 2, 1, 0, 4)
+            if 3 <= i < 7:
+                round_w2(*divmod(i - 3, 2))
+            if i in (5, 7):
+                quantize_w2((i - 5) // 2)
+            if i in (6, 8):
+                weave_d(0, (i - 6) // 2, nc.scalar.copy)
+            if i in (7, 9):
+                quantize_d(0, (i - 7) // 2)
         weave_d(1, 0, nc.vector.tensor_copy)
         weave_d(1, 1, nc.scalar.copy)
 

@@ -127,10 +127,13 @@ def tile_list_breath_peak_scores_kernel(
                 in_=w1_bf[a, b][:, t0:t1, :, :].rearrange("p t m j -> p (t m j)"),
             )
 
-        neg_gain = held([P, 2, PACK], F32, "neg_gain")
+        gain_rows = held([P, 2 * PACK, PK], F32, "gain_rows")
         base_part = held([P, 2, PACK], F32, "base_part")
 
-        nc.scalar.mul(neg_gain[:], gain_sb[:], -1.0)
+        for b in range(2):
+            nc.vector.tensor_copy(
+                out=gain_rows[:, PACK * b : PACK * (b + 1), :], in_=gain_sb[:, b, :].unsqueeze(2).to_broadcast([P, PACK, PK])
+            )
         nc.scalar.mul(base_part[:], base_sb[:], 1.0 / PK)
         gather_words(0)
         gather_plane()
@@ -144,7 +147,8 @@ def tile_list_breath_peak_scores_kernel(
             quantize_w1(1, 0, t, t + 1)
         round_w1(0, 1, 0, nc.scalar.copy)
 
-        d_rows = [held([P, PACK, PK], BF16, f"d_rows{b}") for b in range(2)]
+        timed = [held([P, PACK, PK], F32, f"timed{b}") for b in range(2)]
+        fasting = [held([P, PACK, PK], F32, f"fasting{b}") for b in range(2)]
         d_bf = {}
         d_codes = {(b, c): held([P, HALF], U32, f"d_codes{b}{c}") for b in range(2) for c in range(2)}
         d_plane = {(b, c): held([P, HALF], U8, f"d_plane{b}{c}") for b in range(2) for c in range(2)}
@@ -185,7 +189,7 @@ def tile_list_breath_peak_scores_kernel(
             st = state[i]
             neg_top = held([P, 1], F32, f"neg_top{i}")
             nc.scalar.mul(neg_top[:], st["tops"][:, 1:2], -1.0)
-            a_look = ring.tile([P, PK], F32, name="a_look", align_bytes=64)
+            a_look = ring.tile([P, PK], F32, name="a_look")
             nc.scalar.activation(out=a_look[:], in_=st["h"][:].indirect(p1[:]), func=ACT.Exp, bias=neg_top[:])
             denom = held([P, 1], F32, f"denom{i}")
             terms = ring.tile([P, PK], BF16, name="terms", bufs=2)
@@ -195,10 +199,8 @@ def tile_list_breath_peak_scores_kernel(
             st.update(a=a_look, denom=denom)
 
         def pick(i):
-            st = state[i]
-            fasting = ring.tile([P, PK], F32, name="fasting", bufs=4)
-            nc.vector.tensor_copy(fasting[:], st["h"][:].indirect(p2[:]))
-            st.update(fasting=fasting)
+            b, t = divmod(i, PACK)
+            nc.vector.tensor_tensor(fasting[b][:, t, :], state[i]["h"][:].indirect(p2[:]), gain_rows[:, i, :], ALU.mult)
 
         def invert(i):
             st = state[i]
@@ -209,29 +211,19 @@ def tile_list_breath_peak_scores_kernel(
         def combine(i):
             b, t = divmod(i, PACK)
             st = state[i]
-            inv = st["inv"]
-            timed = ring.tile([P, PK], F32, name="timed")
             nc.vector.scalar_tensor_tensor(
-                out=timed[:], in0=st["a"][:], scalar=inv[:], in1=timing_sb[b][:, t, :], op0=ALU.mult, op1=ALU.mult
-            )
-            st.update(timed=timed)
-
-        def finish(i):
-            b, t = divmod(i, PACK)
-            st = state[i]
-            nc.vector.scalar_tensor_tensor(
-                out=d_rows[b][:, t, :], in0=st["fasting"][:], scalar=neg_gain[:, b, t : t + 1], in1=st["timed"][:],
-                op0=ALU.mult, op1=ALU.add,
+                out=timed[b][:, t, :], in0=st["a"][:], scalar=st["inv"][:], in1=timing_sb[b][:, t, :],
+                op0=ALU.mult, op1=ALU.mult,
             )
 
-        def weave_d(b, c, copy):
-            if (b, c) == (0, 1):
-                d_bf[b, c] = ring.tile([P, HALF, PACK], BF16, name="a_look", align_bytes=64)
-            else:
-                d_bf[b, c] = held([P, HALF, PACK], BF16, f"d_bf{b}{c}")
-            copy(
-                out=d_bf[b, c][:].rearrange("p (g i) t -> p g t i", i=4),
-                in_=d_rows[b][:, :, HALF * c : HALF * (c + 1)].rearrange("p t (g i) -> p g t i", i=4),
+        def finish(b, c):
+            cols = slice(HALF * c, HALF * (c + 1))
+            d_bf[b, c] = ring.tile([P, HALF, PACK], BF16, name="d_bf", bufs=1, align_bytes=64)
+            nc.vector.tensor_tensor(
+                out=d_bf[b, c][:].rearrange("p (g i) t -> p g t i", i=2),
+                in0=timed[b][:, :, cols].rearrange("p t (g i) -> p g t i", i=2),
+                in1=fasting[b][:, :, cols].rearrange("p t (g i) -> p g t i", i=2),
+                op=ALU.subtract,
             )
 
         def quantize_d(b, c):
@@ -260,12 +252,10 @@ def tile_list_breath_peak_scores_kernel(
             if i < 8:
                 empty_bank(i, 1)
                 look(i)
-            if i >= 2:
-                finish(i - 2)
-            if i < 8:
-                pick(i)
             if 1 <= i < 9:
                 invert(i - 1)
+            if i < 8:
+                pick(i)
             if i == 0:
                 round_w1(0, 1, 1, nc.scalar.copy)
             if i in (1, 2):
@@ -276,12 +266,9 @@ def tile_list_breath_peak_scores_kernel(
                 round_w2(*divmod(i - 3, 2))
             if i in (5, 7):
                 quantize_w2((i - 5) // 2)
-            if i in (6, 8):
-                weave_d(0, (i - 6) // 2, nc.scalar.copy)
-            if i in (7, 9):
-                quantize_d(0, (i - 7) // 2)
-        weave_d(1, 0, nc.vector.tensor_copy)
-        weave_d(1, 1, nc.scalar.copy)
+            if i in (7, 8):
+                finish(0, i - 7)
+                quantize_d(0, i - 7)
 
         banks = {}
         for c in range(2):
@@ -314,6 +301,7 @@ def tile_list_breath_peak_scores_kernel(
         second_stage(0, 0)
         second_stage(0, 1)
         for c in range(2):
+            finish(1, c)
             quantize_d(1, c)
             second_stage(1, c)
         for c in range(2):

@@ -152,7 +152,8 @@ def tile_list_breath_peak_scores_kernel(
         d_bf = {}
         d_codes = {(b, c): held([P, HALF], U32, f"d_codes{b}{c}") for b in range(2) for c in range(2)}
         d_plane = {(b, c): held([P, HALF], U8, f"d_plane{b}{c}") for b in range(2) for c in range(2)}
-        w2_bf = [held([P, N, PACK], BF16, f"w2_bf{b}") for b in range(2)]
+        w2_first = held([P, HALF, PACK], BF16, "w2_first")
+        w2_bf = {(0, 0): w2_first[:]}
         w2_codes = [held([P, N], U32, f"w2_codes{b}") for b in range(2)]
         w2_plane = [held([P, N], U8, f"w2_plane{b}") for b in range(2)]
 
@@ -234,13 +235,16 @@ def tile_list_breath_peak_scores_kernel(
         def round_w2(b, c):
             cols = slice(HALF * c, HALF * (c + 1))
             nc.scalar.copy(
-                out=w2_bf[b][:, cols, :].rearrange("p (g i) j -> p g j i", i=4),
+                out=w2_bf[b, c].rearrange("p (g i) j -> p g j i", i=4),
                 in_=w2_raw[b][:, :, cols].rearrange("p j (g i) -> p g j i", i=4),
             )
 
-        def quantize_w2(b):
+        def quantize_w2(b, c):
+            cols = slice(HALF * c, HALF * (c + 1))
             nc.vector.quantize_mx(
-                out=w2_codes[b][:].bitcast(FP8X4), scales=w2_plane[b][:], in_=w2_bf[b][:].rearrange("p n j -> p (n j)")
+                out=w2_codes[b][:, cols].bitcast(FP8X4),
+                scales=w2_plane[b][:, cols],
+                in_=w2_bf[b, c].rearrange("p n j -> p (n j)"),
             )
 
         for i in range(8 + 2):
@@ -262,10 +266,10 @@ def tile_list_breath_peak_scores_kernel(
                 round_w1(1, 1, i - 1, nc.scalar.copy)
             if i in (1, 3):
                 quantize_w1(i // 2, 1, 0, 4)
-            if 3 <= i < 7:
-                round_w2(*divmod(i - 3, 2))
-            if i in (5, 7):
-                quantize_w2((i - 5) // 2)
+            if i == 3:
+                round_w2(0, 0)
+            if i == 5:
+                quantize_w2(0, 0)
             if i in (7, 8):
                 finish(0, i - 7)
                 quantize_d(0, i - 7)
@@ -298,6 +302,11 @@ def tile_list_breath_peak_scores_kernel(
                     stop=(b == 1),
                 )
 
+        w2_late = held([P, 3, HALF, PACK], BF16, "gain_rows")
+        for e, (b, c) in enumerate([(0, 1), (1, 0), (1, 1)]):
+            w2_bf[b, c] = w2_late[:, e, :, :]
+            round_w2(b, c)
+            quantize_w2(b, c)
         second_stage(0, 0)
         second_stage(0, 1)
         for c in range(2):

from contextlib import ExitStack

import concourse.mybir as mybir

K, H, N, T, S, PK = 1024, 1024, 512, 2048, 1024, 512
FLOPS = 2 * K * H * S + 2 * 2 * H * N * PK

F32 = mybir.dt.float32
BF16 = mybir.dt.bfloat16
I32 = mybir.dt.int32
U32 = mybir.dt.uint32
U16 = mybir.dt.uint16
U8 = mybir.dt.uint8
FP8X4 = mybir.dt.float8_e4m3fn_x4
FP4X4 = mybir.dt.float4_e2m1fn_x4
ALU = mybir.AluOpType
ACT = mybir.ActivationFunctionType

P = 128
PACK = 4
KP = P * PACK
HALF = 256


def tile_list_breath_peak_scores_kernel(
    tc, tab_words, tab_scales, offs, pos1, pos2, w1, base, timing, gain, w2, w4_words, w4_scales, out
):
    nc = tc.nc
    with ExitStack() as ctx:
        keep = ctx.enter_context(tc.tile_pool(name="keep", bufs=1))
        ring = ctx.enter_context(tc.tile_pool(name="ring", bufs=3))
        psum = ctx.enter_context(tc.psum_pool(name="psum", bufs=4))

        def held(shape, dtype, name):
            return keep.tile(shape, dtype, name=name, align_bytes=64)

        idx = keep.tile([P, S // 16], U16, name="idx")
        p1 = keep.tile([P, PK // 16], U16, name="p1")
        p2 = keep.tile([P, PK // 16], U16, name="p2")

        tab_plane = held([P, T], U8, "tab_plane")
        w4_plane = held([P, 2, N], U8, "w4_plane")
        nc.vector.memset(tab_plane[:].bitcast(I32), 0)
        nc.vector.memset(w4_plane[:].bitcast(I32), 0)

        def load_tab_plane():
            for q in range(4):
                nc.sync.dma_start(
                    out=tab_plane[32 * q : 32 * q + 8, :].bitcast(I32),
                    in_=tab_scales[:, 4 * q : 4 * q + 4, :].bitcast(I32),
                )

        def load_w4_plane():
            for q in range(4):
                nc.sync.dma_start(
                    out=w4_plane[32 * q : 32 * q + 4, :, :].bitcast(I32),
                    in_=w4_scales[:, 4 * q : 4 * q + 4, :].rearrange("a r c -> r a c").bitcast(I32),
                )

        base_sb = held([P, 2, PACK], F32, "base_sb")
        gain_sb = held([P, 2, PACK], F32, "gain_sb")

        tab = [held([P, T], U32, f"tab{a}") for a in range(2)]
        w1_raw = {(a, b, c): held([P, PACK, HALF], F32, f"w1_raw{a}{b}{c}") for a in range(2) for b in range(2) for c in range(2)}
        w2_raw = [held([P, PACK, N], F32, f"w2_raw{b}") for b in range(2)]
        timing_sb = [held([P, PACK, PK], F32, f"timing{b}") for b in range(2)]
        w4_sb = held([P, 2, 2 * N], U8, "w4_sb")

        def load_tab(a):
            nc.sync.dma_start(out=tab[a][:].bitcast(I32), in_=tab_words[a].rearrange("p t i -> p (t i)").bitcast(I32))

        def load_w1(a, b):
            for c in range(2):
                cols = slice(KP * b + HALF * c, KP * b + HALF * (c + 1))
                nc.sync.dma_start(
                    out=w1_raw[a, b, c][:], in_=w1[KP * a : KP * (a + 1), cols].rearrange("(p j) c -> p j c", j=PACK)
                )

        def load_rows(dst, src, b):
            nc.sync.dma_start(out=dst[b][:], in_=src[KP * b : KP * (b + 1), :].rearrange("(p j) c -> p j c", j=PACK))

        nc.scalar.dma_start(out=gain_sb[:], in_=gain.rearrange("(b p t) -> p b t", b=2, t=PACK))
        nc.scalar.dma_start(out=base_sb[:], in_=base.rearrange("(b p t) -> p b t", b=2, t=PACK))
        nc.sync.dma_start(idx[:], offs)
        load_tab(0)
        nc.sync.dma_start(p1[:], pos1)
        load_tab_plane()
        load_w1(0, 0)
        load_tab(1)
        load_w1(1, 0)
        nc.sync.dma_start(p2[:], pos2)
        load_w1(0, 1)
        load_rows(timing_sb, timing, 0)
        load_w1(1, 1)
        load_rows(timing_sb, timing, 1)
        load_rows(w2_raw, w2, 0)
        load_rows(w2_raw, w2, 1)
        nc.sync.dma_start(out=w4_sb[:].bitcast(I32), in_=w4_words.rearrange("a p c -> p a c").bitcast(I32))
        load_w4_plane()

        v_words = {(a, s): held([P, KP], U32, f"v_words{a}{s}") for a in range(2) for s in range(2)}
        v_plane = [held([P, KP], U8, f"v_plane{s}") for s in range(2)]

        def gather_words(a):
            for s in range(2):
                nc.vector.tensor_copy(v_words[a, s][:], tab[a][:].indirect(idx[:, 32 * s : 32 * (s + 1)]))

        def gather_plane():
            for s in range(2):
                nc.vector.tensor_copy(v_plane[s][:], tab_plane[:].indirect(idx[:, 32 * s : 32 * (s + 1)]))

        w1_bf = {(a, b): held([P, PACK, P, PACK], BF16, f"w1_bf{a}{b}") for a in range(2) for b in range(2)}
        w1_codes = {(a, b): held([P, PACK, P], U32, f"w1_codes{a}{b}") for a in range(2) for b in range(2)}
        w1_plane = {(a, b): held([P, PACK, P], U8, f"w1_plane{a}{b}") for a in range(2) for b in range(2)}

        def round_w1(a, b, c, copy):
            m0 = c * (HALF // PACK)
            copy(
                out=w1_bf[a, b][:, :, m0 : m0 + HALF // PACK, :].rearrange("p t m j -> p m j t"),
                in_=w1_raw[a, b, c][:].rearrange("p j (m t) -> p m j t", t=PACK),
            )

        def quantize_w1(a, b, t0, t1):
            nc.vector.quantize_mx(
                out=w1_codes[a, b][:, t0:t1, :].rearrange("p t m -> p (t m)").bitcast(FP8X4),
                scales=w1_plane[a, b][:, t0:t1, :].rearrange("p t m -> p (t m)"),
                in_=w1_bf[a, b][:, t0:t1, :, :].rearrange("p t m j -> p (t m j)"),
            )

        gain_rows = held([P, 2 * PACK, PK], F32, "gain_rows")
        base_part = held([P, 2, PACK], F32, "base_part")

        for b in range(2):
            nc.vector.tensor_copy(
                out=gain_rows[:, PACK * b : PACK * (b + 1), :], in_=gain_sb[:, b, :].unsqueeze(2).to_broadcast([P, PACK, PK])
            )
        nc.scalar.mul(base_part[:], base_sb[:], 1.0 / PK)
        gather_words(0)
        gather_plane()
        round_w1(0, 0, 0, nc.scalar.copy)
        round_w1(0, 0, 1, nc.scalar.copy)
        quantize_w1(0, 0, 0, 4)
        gather_words(1)
        round_w1(1, 0, 0, nc.scalar.copy)
        round_w1(1, 0, 1, nc.vector.tensor_copy)
        for t in range(PACK):
            quantize_w1(1, 0, t, t + 1)
        round_w1(0, 1, 0, nc.scalar.copy)

        timed = [held([P, PACK, PK], F32, f"timed{b}") for b in range(2)]
        fasting = [held([P, PACK, PK], F32, f"fasting{b}") for b in range(2)]
        d_bf = {}
        d_codes = {(b, c): held([P, HALF], U32, f"d_codes{b}{c}") for b in range(2) for c in range(2)}
        d_plane = {(b, c): held([P, HALF], U8, f"d_plane{b}{c}") for b in range(2) for c in range(2)}
        w2_first = held([P, HALF, PACK], BF16, "w2_first")
        w2_bf = {(0, 0): w2_first[:]}
        w2_codes = [held([P, N], U32, f"w2_codes{b}") for b in range(2)]
        w2_plane = [held([P, N], U8, f"w2_plane{b}") for b in range(2)]

        state = {}

        def first_stage(i):
            b, t = divmod(i, PACK)
            banks = [psum.tile([P, KP], F32, name="h_bank", tag="h_bank") for s in range(2)]
            for a in range(2):
                for s in range(2):
                    nc.tensor.matmul_mx(
                        out=banks[s][:],
                        lhsT=w1_codes[a, b][:, t, :].bitcast(FP8X4),
                        lhsT_scale=w1_plane[a, b][:, t, :],
                        rhs=v_words[a, s][:].bitcast(FP8X4),
                        rhs_scale=v_plane[s][4 * a : P, :],
                        start=(a == 0),
                        stop=(a == 1),
                    )
            h = ring.tile([P, S], F32, name="h", bufs=4)
            tops = held([P, 2], F32, f"tops{i}")
            state[i] = dict(h=h, tops=tops, banks=banks)

        def empty_bank(i, s):
            st = state[i]
            nc.vector.tensor_scalar(
                out=st["h"][:, KP * s : KP * (s + 1)], in0=st["banks"][s][:], scalar1=1.0,
                scalar2=(None if s == 0 else st["tops"][:, 0:1]),
                op0=ALU.mult, op1=ALU.max, accum_out=st["tops"][:, s : s + 1],
            )

        def look(i):
            b, t = divmod(i, PACK)
            st = state[i]
            neg_top = held([P, 1], F32, f"neg_top{i}")
            nc.scalar.mul(neg_top[:], st["tops"][:, 1:2], -1.0)
            a_look = ring.tile([P, PK], F32, name="a_look")
            nc.scalar.activation(out=a_look[:], in_=st["h"][:].indirect(p1[:]), func=ACT.Exp, bias=neg_top[:])
            denom = held([P, 1], F32, f"denom{i}")
            terms = ring.tile([P, PK], BF16, name="terms", bufs=2)
            nc.scalar.activation(
                out=terms[:], in_=a_look[:], func=ACT.Identity, bias=base_part[:, b, t : t + 1], accum_out=denom[:]
            )
            st.update(a=a_look, denom=denom)

        def pick(i):
            b, t = divmod(i, PACK)
            nc.vector.tensor_tensor(fasting[b][:, t, :], state[i]["h"][:].indirect(p2[:]), gain_rows[:, i, :], ALU.mult)

        def invert(i):
            st = state[i]
            inv = held([P, 1], F32, f"inv{i}")
            nc.vector.reciprocal(inv[:], st["denom"][:])
            st.update(inv=inv)

        def combine(i):
            b, t = divmod(i, PACK)
            st = state[i]
            nc.vector.scalar_tensor_tensor(
                out=timed[b][:, t, :], in0=st["a"][:], scalar=st["inv"][:], in1=timing_sb[b][:, t, :],
                op0=ALU.mult, op1=ALU.mult,
            )

        def finish(b, c):
            cols = slice(HALF * c, HALF * (c + 1))
            d_bf[b, c] = ring.tile([P, HALF, PACK], BF16, name="d_bf", bufs=1, align_bytes=64)
            nc.vector.tensor_tensor(
                out=d_bf[b, c][:].rearrange("p (g i) t -> p g t i", i=2),
                in0=timed[b][:, :, cols].rearrange("p t (g i) -> p g t i", i=2),
                in1=fasting[b][:, :, cols].rearrange("p t (g i) -> p g t i", i=2),
                op=ALU.subtract,
            )

        def quantize_d(b, c):
            nc.vector.quantize_mx(
                out=d_codes[b, c][:].bitcast(FP8X4), scales=d_plane[b, c][:], in_=d_bf[b, c][:].rearrange("p m t -> p (m t)")
            )

        def round_w2(b, c):
            cols = slice(HALF * c, HALF * (c + 1))
            nc.scalar.copy(
                out=w2_bf[b, c].rearrange("p (g i) j -> p g j i", i=4),
                in_=w2_raw[b][:, :, cols].rearrange("p j (g i) -> p g j i", i=4),
            )

        def quantize_w2(b, c):
            cols = slice(HALF * c, HALF * (c + 1))
            nc.vector.quantize_mx(
                out=w2_codes[b][:, cols].bitcast(FP8X4),
                scales=w2_plane[b][:, cols],
                in_=w2_bf[b, c].rearrange("p n j -> p (n j)"),
            )

        for i in range(8 + 2):
            if i < 8:
                first_stage(i)
                empty_bank(i, 0)
            if i >= 2:
                combine(i - 2)
            if i < 8:
                empty_bank(i, 1)
                look(i)
            if 1 <= i < 9:
                invert(i - 1)
            if i < 8:
                pick(i)
            if i == 0:
                round_w1(0, 1, 1, nc.scalar.copy)
            if i in (1, 2):
                round_w1(1, 1, i - 1, nc.scalar.copy)
            if i in (1, 3):
                quantize_w1(i // 2, 1, 0, 4)
            if i == 3:
                round_w2(0, 0)
            if i == 5:
                quantize_w2(0, 0)
            if i in (7, 8):
                finish(0, i - 7)
                quantize_d(0, i - 7)

        banks = {}
        for c in range(2):
            for n in range(4):
                tag = "o_bank" if c == 0 else "h_bank"
                banks[c, n] = psum.tile([P, 2, HALF], F32, name=tag, tag=tag)

        def second_stage(b, c):
            for n in range(4):
                cols = slice(P * n, P * (n + 1))
                nc.tensor.matmul_mx(
                    out=banks[c, n][:, 0, :],
                    lhsT=w2_codes[b][:, cols].bitcast(FP8X4),
                    lhsT_scale=w2_plane[b][:, cols],
                    rhs=d_codes[b, c][:].bitcast(FP8X4),
                    rhs_scale=d_plane[b, c][:],
                    start=(b == 0),
                    stop=False,
                )
                nc.tensor.matmul_mx(
                    out=banks[c, n][:, 1, :],
                    lhsT=w4_sb[:, b, 2 * P * n : 2 * P * (n + 1)].bitcast(FP4X4),
                    lhsT_scale=w4_plane[:, b, cols],
                    rhs=d_codes[b, c][:].bitcast(FP8X4),
                    rhs_scale=d_plane[b, c][:],
                    start=False,
                    stop=(b == 1),
                )

        w2_late = held([P, 3, HALF, PACK], BF16, "gain_rows")
        for e, (b, c) in enumerate([(0, 1), (1, 0), (1, 1)]):
            w2_bf[b, c] = w2_late[:, e, :, :]
            round_w2(b, c)
            quantize_w2(b, c)
        second_stage(0, 0)
        second_stage(0, 1)
        for c in range(2):
            finish(1, c)
            quantize_d(1, c)
            second_stage(1, c)
        for c in range(2):
            for n in range(4):
                early = ring.tile([P, HALF], F32, name="early", bufs=4)
                nc.scalar.copy(out=early[:], in_=banks[c, n][:, 0, :])
                score = ring.tile([P, HALF], F32, name="score", bufs=8)
                nc.vector.tensor_tensor(out=score[:], in0=banks[c, n][:, 1, :], in1=early[:], op=ALU.min)
                nc.sync.dma_start(out=out[P * n : P * (n + 1), HALF * c : HALF * (c + 1)], in_=score[:])
